import numpy as np
import ml_dtypes


def mxq(x, axis, fmt="e4m3"):
    dtype, down = {"e4m3": (ml_dtypes.float8_e4m3fn, 7), "e5m2": (ml_dtypes.float8_e5m2, 14)}[fmt]
    v = np.moveaxis(np.asarray(x, np.float32).astype(ml_dtypes.bfloat16).astype(np.float64), axis, -1)
    blocks = v.reshape(v.shape[:-1] + (-1, 32))
    amax = np.abs(blocks).max(-1, keepdims=True)
    byte = np.maximum(np.where(amax > 0, np.frexp(amax)[1] - 1 + 127, 0) - down, 1)
    scale = np.exp2(byte - 127.0)
    codes = (blocks / scale).astype(np.float32).astype(dtype).astype(np.float64)
    return np.moveaxis((codes * scale).reshape(v.shape), -1, axis)


WIDE = False


def mx_kscale(k):
    if not WIDE:
        return np.ones(k)
    levels = np.array([10, -10, 5, -5, 0])
    if k % 512:
        return np.exp2(np.random.permutation(np.resize(levels, k // 32))).repeat(32)
    a = np.empty((k // 512, 16))
    for p in range(k // 512):
        a[p, :8] = np.random.permutation(np.resize(levels, 8))
        for g in range(8):
            far = levels[np.abs(levels - a[p, g]) >= 10]
            a[p, g + 8] = far[np.random.randint(len(far))]
    return np.exp2(a.ravel()).repeat(32)


def f64(x):
    return np.asarray(x).astype(np.float64)


def striped8(idx):
    return np.asarray(idx).reshape(8, -1, 16).transpose(0, 2, 1).reshape(128, -1).astype(np.uint16)


def unstriped8(offs):
    return offs.reshape(8, 16, -1).transpose(0, 2, 1).reshape(8, -1).astype(np.int64)


def pick8(x, idx, run):
    r = np.arange(len(x))
    return x[r[:, None], idx[r % (8 * run) // run]]


E2M1 = np.array([0.0, 0.5, 1.0, 1.5, 2.0, 3.0, 4.0, 6.0, -0.0, -0.5, -1.0, -1.5, -2.0, -3.0, -4.0, -6.0])


def pack_weight(w, fmt):
    k, n = w.shape
    w = f64(np.asarray(w, np.float32).astype(ml_dtypes.bfloat16)).reshape(k // 32, 32, n)
    amax = np.abs(w).max(1)
    if fmt == "e4m3":
        byte = np.frexp(amax)[1] - 1 + 127 - 7
    else:
        mant, ex = np.frexp(amax / 6.0)
        byte = np.where(mant > 0.5, ex, ex - 1) + 127
    byte = np.clip(np.where(amax > 0, byte, 1), 1, 254)
    scaled = (w * np.exp2(127.0 - byte)[:, None, :]).reshape(k, n).astype(np.float32)
    by_word = np.ascontiguousarray(scaled.reshape(k // 512, 128, 4, n).transpose(0, 1, 3, 2))
    if fmt == "e4m3":
        words = by_word.astype(ml_dtypes.float8_e4m3fn).view(np.uint8)
    else:
        c = by_word.astype(ml_dtypes.float4_e2m1fn).view(np.uint8) & 0xF
        words = (c[..., 0::2] | (c[..., 1::2] << 4)).reshape(k // 512, 128, 2 * n)
    return np.ascontiguousarray(words), np.ascontiguousarray(byte.astype(np.uint8).reshape(k // 512, 16, n))


def unpack_weight(words, scales, fmt):
    g, _, n = scales.shape
    words = np.ascontiguousarray(words).reshape(g, 128, n, -1)
    if fmt == "e4m3":
        vals = words.view(ml_dtypes.float8_e4m3fn).astype(np.float64)
    else:
        nib = np.empty((g, 128, n, 4), np.uint8)
        nib[..., 0::2] = words & 0xF
        nib[..., 1::2] = words >> 4
        vals = E2M1[nib]
    vals = vals * np.repeat(np.exp2(scales.astype(np.float64) - 127.0), 8, axis=1)[..., None]
    return vals.transpose(0, 1, 3, 2).reshape(g * 512, n)


D, K, T, U, X, Z, I, J, M, Q = 512, 512, 1024, 512, 512, 1024, 512, 256, 128, 128


def setup_inputs():
    n = np.random.standard_normal
    idx = np.stack([np.random.permutation(T)[:J] for _ in range(8)])
    idx2 = np.stack([np.random.permutation(U)[:M] for _ in range(8)])
    idx3 = np.stack([np.random.permutation(X)[:M] for _ in range(8)])
    idx4 = np.stack([np.random.permutation(Z)[:I] for _ in range(8)])
    idx5 = np.stack([np.random.permutation(Z)[:I] for _ in range(8)])
    fd = mx_kscale(D)
    fk = mx_kscale(K)
    wqp = pack_weight(n((D, K)) * 1.0 / np.sqrt(D) * fd[:, None] * fk, "e4m3")
    cachep = pack_weight(n((K, T)) * 1.0 / np.sqrt(K) / fk[:, None], "e4m3")
    draftp = pack_weight(n((K, U)) * 1.0 / np.sqrt(K) / fk[:, None], "e2m1")
    archp = pack_weight(n((D, X)) * 1.0 / np.sqrt(D) * fd[:, None], "e4m3")
    return {
        "states": (n((D, Q)) * 0.95 / fd[:, None]).astype(np.float32),
        "wq_words": wqp[0],
        "wq_scales": wqp[1],
        "cache_words": cachep[0],
        "cache_scales": cachep[1],
        "draft_words": draftp[0],
        "draft_scales": draftp[1],
        "arch_words": archp[0],
        "arch_scales": archp[1],
        "offs": striped8(idx),
        "offs2": striped8(idx2),
        "offs3": striped8(idx3),
        "offs4": striped8(idx4),
        "offs5": striped8(idx5),
    }


def reference(states, wq_words, wq_scales, cache_words, cache_scales, draft_words, draft_scales, arch_words, arch_scales, offs, offs2, offs3, offs4, offs5):
    idx = unstriped8(offs)
    idx2 = unstriped8(offs2)
    idx3 = unstriped8(offs3)
    idx4 = unstriped8(offs4)
    idx5 = unstriped8(offs5)
    wqu = unpack_weight(wq_words, wq_scales, "e4m3")
    cacheu = unpack_weight(cache_words, cache_scales, "e4m3")
    draftu = unpack_weight(draft_words, draft_scales, "e2m1")
    archu = unpack_weight(arch_words, arch_scales, "e4m3")
    statesq = mxq(f64(states), 0, "e4m3")
    qv = wqu.T @ statesq
    qvq = mxq(qv, 0, "e4m3")
    a = qvq.T @ cacheu
    b = qvq.T @ draftu
    c0 = statesq.T @ archu
    v = np.concatenate([pick8(b, idx2, 16), pick8(c0, idx3, 16)], axis=1)
    w = np.concatenate([pick8(a, idx, 16), v], axis=1)
    f1 = np.zeros((Q, Z))
    f1[np.arange(Q)[:, None], idx4[np.arange(Q) % 128 // 16]] = w
    y = np.maximum(pick8(f1, idx5, 16), w)
    return y

@@ -1,0 +1,189 @@
+from contextlib import ExitStack
+
+import concourse.mybir as mybir
+
+FLOPS = 335544320
+
+F32 = mybir.dt.float32
+BF16 = mybir.dt.bfloat16
+I32 = mybir.dt.int32
+U32 = mybir.dt.uint32
+U16 = mybir.dt.uint16
+U8 = mybir.dt.uint8
+FP8X4 = mybir.dt.float8_e4m3fn_x4
+FP4X4 = mybir.dt.float4_e2m1fn_x4
+COPY = mybir.ActivationFunctionType.Copy
+
+P = 128
+PACK = 4
+Q = 128
+K = 512
+T = 1024
+U = 512
+X = 512
+Z = 1024
+SLOTS = 512
+PIECE = 256
+
+
+def tile_attend_raggedthree_sidethree_kernel(
+    tc, states, wq_words, wq_scales, cache_words, cache_scales, draft_words, draft_scales,
+    arch_words, arch_scales, offs, offs2, offs3, offs4, offs5, out,
+):
+    nc = tc.nc
+    with ExitStack() as ctx:
+        sb = ctx.enter_context(tc.tile_pool(name="sb", bufs=1))
+        scores = ctx.enter_context(tc.tile_pool(name="scores", bufs=1))
+        ps = ctx.enter_context(tc.psum_pool(name="ps", bufs=1))
+
+        def load_scale_rows(queue, name, scales, rows=None):
+            width = scales.shape[2]
+            if rows is None:
+                rows = sb.tile([4, 4, width // 4], I32, name=name)
+            queue.dma_start(rows[:], scales[0].bitcast(I32).rearrange("(g r) n -> r g n", r=4))
+            return rows
+
+        def zeroed_plane(name, width):
+            plane = sb.tile([P, width], U8, name=name, align_bytes=64)
+            nc.vector.memset(plane[:].bitcast(I32), 0)
+            return plane
+
+        def spread_scale_rows(plane, rows, share=True):
+            if share:
+                nc.scalar.copy(plane[0:4, :].bitcast(U32), rows[:, 0, :].bitcast(U32))
+            for g in range(1 if share else 0, 4):
+                nc.vector.tensor_copy(plane[32 * g : 32 * g + 4, :].bitcast(I32), rows[:, g, :])
+
+        def load_words(name, words_2d):
+            held = sb.tile([P, words_2d.shape[1]], U8, name=name, align_bytes=64)
+            nc.sync.dma_start(held[:].bitcast(I32), words_2d.bitcast(I32))
+            return held
+
+        def load_list(name, lists):
+            held = sb.tile([P, lists.shape[1]], U16, name=name)
+            nc.sync.dma_start(held[:], lists)
+            return held
+
+        wq_rows = load_scale_rows(nc.scalar, "wq_rows", wq_scales)
+        st_raw = sb.tile([P, PACK, Q], F32, name="st_raw")
+        nc.sync.dma_start(st_raw[:], states.rearrange("(p j) q -> p j q", j=PACK))
+        wq_w = load_words("wq_w", wq_words[0].rearrange("p n t -> p (n t)"))
+        arch_rows = load_scale_rows(nc.sync, "arch_rows", arch_scales)
+        arch_w = load_words("arch_w", arch_words[0].rearrange("p n t -> p (n t)"))
+        draft_rows = load_scale_rows(nc.sync, "draft_rows", draft_scales)
+        cache_rows = scores.tile([4, 4, T // 4], I32, name="cache_rows", offset=0, align_bytes=64)
+        load_scale_rows(nc.sync, "cache_rows", cache_scales, cache_rows)
+        draft_w = load_words("draft_w", draft_words[0])
+        cache_w = load_words("cache_w", cache_words[0].rearrange("p n t -> p (n t)"))
+        list_put = load_list("list_put", offs4)
+        list_b = load_list("list_b", offs2)
+        list_c = load_list("list_c", offs3)
+        list_a = load_list("list_a", offs)
+        list_get = load_list("list_get", offs5)
+
+        wq_plane = zeroed_plane("wq_plane", K)
+        arch_plane = zeroed_plane("arch_plane", X)
+        cache_plane = zeroed_plane("cache_plane", T)
+        draft_plane = zeroed_plane("draft_plane", U)
+        page = sb.tile([P, Z], F32, name="page")
+        nc.gpsimd.memset(page[:], 0.0)
+
+        spread_scale_rows(wq_plane, wq_rows, share=False)
+        st_bf = sb.tile([P, Q, PACK], BF16, name="st_bf", align_bytes=64)
+        nc.vector.tensor_copy(
+            st_bf[:].rearrange("p (c i) j -> p c j i", i=4),
+            st_raw[:].rearrange("p j (c i) -> p c j i", i=4),
+        )
+        wq_plane_dealt = sb.tile([P, PACK, P], U8, name="wq_plane_dealt", align_bytes=64)
+        plane_by_t = wq_plane[:].rearrange("p (m t) -> p t m", t=PACK)
+        nc.vector.tensor_copy(wq_plane_dealt[:, 0:2, :], plane_by_t[:, 0:2, :])
+        st_codes = sb.tile([P, Q], U32, name="st_codes", align_bytes=64)
+        st_plane = sb.tile([P, Q], U8, name="st_plane", align_bytes=64)
+        nc.vector.quantize_mx(st_codes[:].bitcast(FP8X4), st_plane[:], st_bf[:].rearrange("p q j -> p (q j)"))
+        nc.vector.tensor_copy(wq_plane_dealt[:, 2:4, :], plane_by_t[:, 2:4, :])
+
+        wq_dealt = sb.tile([P, PACK, P], U32, name="wq_dealt", align_bytes=64)
+        for t in (0, 2):
+            nc.scalar.copy(
+                wq_dealt[:, t : t + 2, :].rearrange("p t m -> p m t"),
+                wq_w[:].bitcast(U32).rearrange("p (m t) -> p m t", t=PACK)[:, :, t : t + 2],
+            )
+
+        qv_ps = ps.tile([P, PACK, Q], F32, name="qv_ps", tag="first_and_last")
+        for t in range(PACK):
+            nc.tensor.matmul_mx(
+                qv_ps[:, t, :],
+                lhsT=wq_dealt[:, t, :].bitcast(FP8X4), lhsT_scale=wq_plane_dealt[:, t, :],
+                rhs=st_codes[:].bitcast(FP8X4), rhs_scale=st_plane[:],
+                start=True, stop=True,
+            )
+
+        spread_scale_rows(arch_plane, arch_rows)
+        c_ps = []
+        for i in range(X // PIECE):
+            cols = slice(i * PIECE, (i + 1) * PIECE)
+            c_ps.append(ps.tile([P, PIECE], F32, name="c_ps%d" % i))
+            nc.tensor.matmul_mx(
+                c_ps[i][:],
+                lhsT=st_codes[:].bitcast(FP8X4), lhsT_scale=st_plane[:],
+                rhs=arch_w[:, 4 * cols.start : 4 * cols.stop].bitcast(FP8X4), rhs_scale=arch_plane[:, cols],
+                start=True, stop=True,
+            )
+        spread_scale_rows(draft_plane, draft_rows)
+        spread_scale_rows(cache_plane, cache_rows)
+
+        qv_bf = scores.tile([P, Q, PACK], BF16, name="qv_bf", offset=512, align_bytes=64)
+        nc.scalar.copy(qv_bf[:], qv_ps[:].rearrange("p t q -> p q t"))
+        c_sb = scores.tile([P, X], F32, name="c_sb", offset=1536)
+        nc.vector.tensor_copy(c_sb[:, :PIECE], c_ps[0][:])
+        nc.vector.tensor_copy(c_sb[:, PIECE:], c_ps[1][:])
+        qv_codes = scores.tile([P, Q], U32, name="qv_codes", offset=0, align_bytes=64)
+        qv_plane = sb.tile([P, Q], U8, name="qv_plane", align_bytes=64)
+        nc.vector.quantize_mx(qv_codes[:].bitcast(FP8X4), qv_plane[:], qv_bf[:].rearrange("p q t -> p (q t)"))
+
+        w = sb.tile([P, SLOTS], F32, name="w")
+        nc.vector.tensor_copy(w[:, 384:512], c_sb[:].indirect(list_c[:]))
+
+        nc.scalar.activation(page[:].indirect(list_put[:, 24:32]), w[:, 384:512], COPY)
+
+        b_sb = scores.tile([P, U], F32, name="b_sb", offset=512)
+        for i in range(U // PIECE):
+            cols = slice(i * PIECE, (i + 1) * PIECE)
+            b_ps = ps.tile([P, PIECE], F32, name="b_ps%d" % i)
+            nc.tensor.matmul_mx(
+                b_ps[:],
+                lhsT=qv_codes[:].bitcast(FP8X4), lhsT_scale=qv_plane[:],
+                rhs=draft_w[:, 2 * cols.start : 2 * cols.stop].bitcast(FP4X4), rhs_scale=draft_plane[:, cols],
+                start=True, stop=True,
+            )
+            nc.vector.tensor_copy(b_sb[:, cols], b_ps[:])
+        nc.vector.tensor_copy(w[:, 256:384], b_sb[:].indirect(list_b[:]))
+
+        a_sb = scores.tile([P, T], F32, name="a_sb", offset=2560)
+        for i in range(T // PIECE):
+            cols = slice(i * PIECE, (i + 1) * PIECE)
+            a_ps = ps.tile([P, PIECE], F32, name="a_ps%d" % i, tag="first_and_last" if i == 3 else "a_ps%d" % i)
+            nc.tensor.matmul_mx(
+                a_ps[:],
+                lhsT=qv_codes[:].bitcast(FP8X4), lhsT_scale=qv_plane[:],
+                rhs=cache_w[:, 4 * cols.start : 4 * cols.stop].bitcast(FP8X4), rhs_scale=cache_plane[:, cols],
+                start=True, stop=True,
+            )
+            if i < 2:
+                nc.scalar.copy(a_sb[:, cols], a_ps[:])
+            else:
+                nc.vector.tensor_copy(a_sb[:, cols], a_ps[:])
+        nc.scalar.activation(page[:].indirect(list_put[:, 16:24]), w[:, 256:384], COPY)
+        nc.vector.tensor_copy(w[:, 0:256], a_sb[:].indirect(list_a[:]))
+        nc.scalar.activation(page[:].indirect(list_put[:, 0:16]), w[:, 0:256], COPY)
+
+        got_lo = sb.tile([P, 256], F32, name="got_lo")
+        got_hi = sb.tile([P, 256], F32, name="got_hi")
+        nc.vector.tensor_copy(got_lo[:], page[:].indirect(list_get[:, 0:16]))
+        nc.scalar.activation(got_hi[:], page[:].indirect(list_get[:, 16:32]), COPY)
+        res_lo = sb.tile([P, 256], F32, name="res_lo")
+        res_hi = sb.tile([P, 256], F32, name="res_hi")
+        nc.vector.tensor_max(res_lo[:], got_lo[:], w[:, 0:256])
+        nc.sync.dma_start(out[:, 0:256], res_lo[:])
+        nc.vector.tensor_max(res_hi[:], got_hi[:], w[:, 256:512])
+        nc.scalar.dma_start(out[:, 256:512], res_hi[:])

@@ -48,10 +48,8 @@ def tile_attend_raggedthree_sidethree_kernel(
             nc.vector.memset(plane[:].bitcast(I32), 0)
             return plane
 
-        def spread_scale_rows(plane, rows, share=True):
-            if share:
-                nc.scalar.copy(plane[0:4, :].bitcast(U32), rows[:, 0, :].bitcast(U32))
-            for g in range(1 if share else 0, 4):
+        def spread_scale_rows(plane, rows, first=0):
+            for g in range(first, 4):
                 nc.vector.tensor_copy(plane[32 * g : 32 * g + 4, :].bitcast(I32), rows[:, g, :])
 
         def load_words(name, words_2d):
@@ -70,25 +68,31 @@ def tile_attend_raggedthree_sidethree_kernel(
         wq_w = load_words("wq_w", wq_words[0].rearrange("p n t -> p (n t)"))
         arch_rows = load_scale_rows(nc.sync, "arch_rows", arch_scales)
         arch_w = load_words("arch_w", arch_words[0].rearrange("p n t -> p (n t)"))
-        draft_rows = load_scale_rows(nc.sync, "draft_rows", draft_scales)
-        cache_rows = scores.tile([4, 4, T // 4], I32, name="cache_rows", offset=0, align_bytes=64)
-        load_scale_rows(nc.sync, "cache_rows", cache_scales, cache_rows)
-        draft_w = load_words("draft_w", draft_words[0])
-        cache_w = load_words("cache_w", cache_words[0].rearrange("p n t -> p (n t)"))
+        draft_rows = scores.tile([4, 4, U // 4], I32, name="draft_rows", offset=0, align_bytes=64)
+        load_scale_rows(nc.sync, "draft_rows", draft_scales, draft_rows)
         list_put = load_list("list_put", offs4)
-        list_b = load_list("list_b", offs2)
         list_c = load_list("list_c", offs3)
+        draft_w = load_words("draft_w", draft_words[0])
+        cache_bytes = cache_words[0].rearrange("p n t -> p (n t)")
+        cache_w = load_words("cache_w", cache_bytes[:, : 12 * PIECE])
+        cache_plane = zeroed_plane("cache_plane", PIECE)
+        cache_by_piece = cache_scales[0].bitcast(I32).rearrange("f (j n) -> j f n", j=4)
+        for g in range(4):
+            nc.sync.dma_start(
+                cache_plane[32 * g : 32 * g + 16, :].bitcast(I32), cache_by_piece[:, 4 * g : 4 * g + 4, :]
+            )
+        list_b = load_list("list_b", offs2)
+        cache_last_w = load_words("cache_last_w", cache_bytes[:, 12 * PIECE :])
         list_a = load_list("list_a", offs)
         list_get = load_list("list_get", offs5)
 
         wq_plane = zeroed_plane("wq_plane", K)
         arch_plane = zeroed_plane("arch_plane", X)
-        cache_plane = zeroed_plane("cache_plane", T)
         draft_plane = zeroed_plane("draft_plane", U)
         page = sb.tile([P, Z], F32, name="page")
         nc.gpsimd.memset(page[:], 0.0)
 
-        spread_scale_rows(wq_plane, wq_rows, share=False)
+        spread_scale_rows(wq_plane, wq_rows)
         st_bf = sb.tile([P, Q, PACK], BF16, name="st_bf", align_bytes=64)
         nc.vector.tensor_copy(
             st_bf[:].rearrange("p (c i) j -> p c j i", i=4),
@@ -118,7 +122,8 @@ def tile_attend_raggedthree_sidethree_kernel(
                 start=True, stop=True,
             )
 
-        spread_scale_rows(arch_plane, arch_rows)
+        nc.scalar.copy(arch_plane[0:4, :].bitcast(U32), arch_rows[:, 0, :].bitcast(U32))
+        spread_scale_rows(arch_plane, arch_rows, first=1)
         c_ps = []
         for i in range(X // PIECE):
             cols = slice(i * PIECE, (i + 1) * PIECE)
@@ -130,11 +135,10 @@ def tile_attend_raggedthree_sidethree_kernel(
                 start=True, stop=True,
             )
         spread_scale_rows(draft_plane, draft_rows)
-        spread_scale_rows(cache_plane, cache_rows)
 
-        qv_bf = scores.tile([P, Q, PACK], BF16, name="qv_bf", offset=512, align_bytes=64)
+        qv_bf = sb.tile([P, Q, PACK], BF16, name="qv_bf", align_bytes=64)
         nc.scalar.copy(qv_bf[:], qv_ps[:].rearrange("p t q -> p q t"))
-        c_sb = scores.tile([P, X], F32, name="c_sb", offset=1536)
+        c_sb = scores.tile([P, X], F32, name="c_sb", offset=512)
         nc.vector.tensor_copy(c_sb[:, :PIECE], c_ps[0][:])
         nc.vector.tensor_copy(c_sb[:, PIECE:], c_ps[1][:])
         qv_codes = scores.tile([P, Q], U32, name="qv_codes", offset=0, align_bytes=64)
@@ -146,7 +150,7 @@ def tile_attend_raggedthree_sidethree_kernel(
 
         nc.scalar.activation(page[:].indirect(list_put[:, 24:32]), w[:, 384:512], COPY)
 
-        b_sb = scores.tile([P, U], F32, name="b_sb", offset=512)
+        b_sb = sb.tile([P, U], F32, name="b_sb")
         for i in range(U // PIECE):
             cols = slice(i * PIECE, (i + 1) * PIECE)
             b_ps = ps.tile([P, PIECE], F32, name="b_ps%d" % i)
@@ -159,14 +163,14 @@ def tile_attend_raggedthree_sidethree_kernel(
             nc.vector.tensor_copy(b_sb[:, cols], b_ps[:])
         nc.vector.tensor_copy(w[:, 256:384], b_sb[:].indirect(list_b[:]))
 
-        a_sb = scores.tile([P, T], F32, name="a_sb", offset=2560)
+        a_sb = sb.tile([P, T], F32, name="a_sb")
         for i in range(T // PIECE):
             cols = slice(i * PIECE, (i + 1) * PIECE)
             a_ps = ps.tile([P, PIECE], F32, name="a_ps%d" % i, tag="first_and_last" if i == 3 else "a_ps%d" % i)
             nc.tensor.matmul_mx(
                 a_ps[:],
                 lhsT=qv_codes[:].bitcast(FP8X4), lhsT_scale=qv_plane[:],
-                rhs=cache_w[:, 4 * cols.start : 4 * cols.stop].bitcast(FP8X4), rhs_scale=cache_plane[:, cols],
+                rhs=(cache_w[:, 4 * cols.start : 4 * cols.stop] if i < 3 else cache_last_w[:]).bitcast(FP8X4), rhs_scale=cache_plane[4 * i :, :],
                 start=True, stop=True,
             )
             if i < 2:

@@ -62,7 +62,7 @@ def tile_attend_raggedthree_sidethree_kernel(
             nc.sync.dma_start(held[:], lists)
             return held
 
-        wq_rows = load_scale_rows(nc.scalar, "wq_rows", wq_scales)
+        wq_rows = load_scale_rows(nc.sync, "wq_rows", wq_scales)
         st_raw = sb.tile([P, PACK, Q], F32, name="st_raw")
         nc.sync.dma_start(st_raw[:], states.rearrange("(p j) q -> p j q", j=PACK))
         wq_w = load_words("wq_w", wq_words[0].rearrange("p n t -> p (n t)"))
@@ -173,7 +173,7 @@ def tile_attend_raggedthree_sidethree_kernel(
                 rhs=(cache_w[:, 4 * cols.start : 4 * cols.stop] if i < 3 else cache_last_w[:]).bitcast(FP8X4), rhs_scale=cache_plane[4 * i :, :],
                 start=True, stop=True,
             )
-            if i < 2:
+            if i in (1, 2):
                 nc.scalar.copy(a_sb[:, cols], a_ps[:])
             else:
                 nc.vector.tensor_copy(a_sb[:, cols], a_ps[:])

@@ -68,6 +68,16 @@ def tile_attend_raggedthree_sidethree_kernel(
         wq_w = load_words("wq_w", wq_words[0].rearrange("p n t -> p (n t)"))
         arch_rows = load_scale_rows(nc.sync, "arch_rows", arch_scales)
         arch_w = load_words("arch_w", arch_words[0].rearrange("p n t -> p (n t)"))
+        cache_plane = zeroed_plane("cache_plane", PIECE)
+        cache_by_piece = cache_scales[0].bitcast(I32).rearrange("f (j n) -> j f n", j=4)
+
+        def load_cache_quadrant(g):
+            nc.sync.dma_start(
+                cache_plane[32 * g : 32 * g + 16, :].bitcast(I32), cache_by_piece[:, 4 * g : 4 * g + 4, :]
+            )
+
+        load_cache_quadrant(0)
+        load_cache_quadrant(1)
         draft_rows = scores.tile([4, 4, U // 4], I32, name="draft_rows", offset=0, align_bytes=64)
         load_scale_rows(nc.sync, "draft_rows", draft_scales, draft_rows)
         list_put = load_list("list_put", offs4)
@@ -75,12 +85,8 @@ def tile_attend_raggedthree_sidethree_kernel(
         draft_w = load_words("draft_w", draft_words[0])
         cache_bytes = cache_words[0].rearrange("p n t -> p (n t)")
         cache_w = load_words("cache_w", cache_bytes[:, : 12 * PIECE])
-        cache_plane = zeroed_plane("cache_plane", PIECE)
-        cache_by_piece = cache_scales[0].bitcast(I32).rearrange("f (j n) -> j f n", j=4)
-        for g in range(4):
-            nc.sync.dma_start(
-                cache_plane[32 * g : 32 * g + 16, :].bitcast(I32), cache_by_piece[:, 4 * g : 4 * g + 4, :]
-            )
+        load_cache_quadrant(2)
+        load_cache_quadrant(3)
         list_b = load_list("list_b", offs2)
         cache_last_w = load_words("cache_last_w", cache_bytes[:, 12 * PIECE :])
         list_a = load_list("list_a", offs)
@@ -140,7 +146,7 @@ def tile_attend_raggedthree_sidethree_kernel(
         nc.scalar.copy(qv_bf[:], qv_ps[:].rearrange("p t q -> p q t"))
         c_sb = scores.tile([P, X], F32, name="c_sb", offset=512)
         nc.vector.tensor_copy(c_sb[:, :PIECE], c_ps[0][:])
-        nc.vector.tensor_copy(c_sb[:, PIECE:], c_ps[1][:])
+        nc.scalar.copy(c_sb[:, PIECE:], c_ps[1][:])
         qv_codes = scores.tile([P, Q], U32, name="qv_codes", offset=0, align_bytes=64)
         qv_plane = sb.tile([P, Q], U8, name="qv_plane", align_bytes=64)
         nc.vector.quantize_mx(qv_codes[:].bitcast(FP8X4), qv_plane[:], qv_bf[:].rearrange("p q t -> p (q t)"))

from contextlib import ExitStack

import concourse.mybir as mybir

FLOPS = 335544320

F32 = mybir.dt.float32
BF16 = mybir.dt.bfloat16
I32 = mybir.dt.int32
U32 = mybir.dt.uint32
U16 = mybir.dt.uint16
U8 = mybir.dt.uint8
FP8X4 = mybir.dt.float8_e4m3fn_x4
FP4X4 = mybir.dt.float4_e2m1fn_x4
COPY = mybir.ActivationFunctionType.Copy

P = 128
PACK = 4
Q = 128
K = 512
T = 1024
U = 512
X = 512
Z = 1024
SLOTS = 512
PIECE = 256


def tile_attend_raggedthree_sidethree_kernel(
    tc, states, wq_words, wq_scales, cache_words, cache_scales, draft_words, draft_scales,
    arch_words, arch_scales, offs, offs2, offs3, offs4, offs5, out,
):
    nc = tc.nc
    with ExitStack() as ctx:
        sb = ctx.enter_context(tc.tile_pool(name="sb", bufs=1))
        scores = ctx.enter_context(tc.tile_pool(name="scores", bufs=1))
        ps = ctx.enter_context(tc.psum_pool(name="ps", bufs=1))

        def load_scale_rows(queue, name, scales, rows=None):
            width = scales.shape[2]
            if rows is None:
                rows = sb.tile([4, 4, width // 4], I32, name=name)
            queue.dma_start(rows[:], scales[0].bitcast(I32).rearrange("(g r) n -> r g n", r=4))
            return rows

        def zeroed_plane(name, width):
            plane = sb.tile([P, width], U8, name=name, align_bytes=64)
            nc.vector.memset(plane[:].bitcast(I32), 0)
            return plane

        def spread_scale_rows(plane, rows, first=0):
            for g in range(first, 4):
                nc.vector.tensor_copy(plane[32 * g : 32 * g + 4, :].bitcast(I32), rows[:, g, :])

        def load_words(name, words_2d):
            held = sb.tile([P, words_2d.shape[1]], U8, name=name, align_bytes=64)
            nc.sync.dma_start(held[:].bitcast(I32), words_2d.bitcast(I32))
            return held

        def load_list(name, lists):
            held = sb.tile([P, lists.shape[1]], U16, name=name)
            nc.sync.dma_start(held[:], lists)
            return held

        wq_rows = load_scale_rows(nc.sync, "wq_rows", wq_scales)
        st_raw = sb.tile([P, PACK, Q], F32, name="st_raw")
        nc.sync.dma_start(st_raw[:], states.rearrange("(p j) q -> p j q", j=PACK))
        wq_w = load_words("wq_w", wq_words[0].rearrange("p n t -> p (n t)"))
        arch_rows = load_scale_rows(nc.sync, "arch_rows", arch_scales)
        arch_w = load_words("arch_w", arch_words[0].rearrange("p n t -> p (n t)"))
        cache_plane = zeroed_plane("cache_plane", PIECE)
        cache_by_piece = cache_scales[0].bitcast(I32).rearrange("f (j n) -> j f n", j=4)

        def load_cache_quadrant(g):
            nc.sync.dma_start(
                cache_plane[32 * g : 32 * g + 16, :].bitcast(I32), cache_by_piece[:, 4 * g : 4 * g + 4, :]
            )

        load_cache_quadrant(0)
        load_cache_quadrant(1)
        draft_rows = scores.tile([4, 4, U // 4], I32, name="draft_rows", offset=0, align_bytes=64)
        load_scale_rows(nc.sync, "draft_rows", draft_scales, draft_rows)
        list_put = load_list("list_put", offs4)
        list_c = load_list("list_c", offs3)
        draft_w = load_words("draft_w", draft_words[0])
        cache_bytes = cache_words[0].rearrange("p n t -> p (n t)")
        cache_w = load_words("cache_w", cache_bytes[:, : 12 * PIECE])
        load_cache_quadrant(2)
        load_cache_quadrant(3)
        list_b = load_list("list_b", offs2)
        cache_last_w = load_words("cache_last_w", cache_bytes[:, 12 * PIECE :])
        list_a = load_list("list_a", offs)
        list_get = load_list("list_get", offs5)

        wq_plane = zeroed_plane("wq_plane", K)
        arch_plane = zeroed_plane("arch_plane", X)
        draft_plane = zeroed_plane("draft_plane", U)
        page = sb.tile([P, Z], F32, name="page")
        nc.gpsimd.memset(page[:], 0.0)

        spread_scale_rows(wq_plane, wq_rows)
        st_bf = sb.tile([P, Q, PACK], BF16, name="st_bf", align_bytes=64)
        nc.vector.tensor_copy(
            st_bf[:].rearrange("p (c i) j -> p c j i", i=4),
            st_raw[:].rearrange("p j (c i) -> p c j i", i=4),
        )
        wq_plane_dealt = sb.tile([P, PACK, P], U8, name="wq_plane_dealt", align_bytes=64)
        plane_by_t = wq_plane[:].rearrange("p (m t) -> p t m", t=PACK)
        nc.vector.tensor_copy(wq_plane_dealt[:, 0:2, :], plane_by_t[:, 0:2, :])
        st_codes = sb.tile([P, Q], U32, name="st_codes", align_bytes=64)
        st_plane = sb.tile([P, Q], U8, name="st_plane", align_bytes=64)
        nc.vector.quantize_mx(st_codes[:].bitcast(FP8X4), st_plane[:], st_bf[:].rearrange("p q j -> p (q j)"))
        nc.vector.tensor_copy(wq_plane_dealt[:, 2:4, :], plane_by_t[:, 2:4, :])

        wq_dealt = sb.tile([P, PACK, P], U32, name="wq_dealt", align_bytes=64)
        for t in (0, 2):
            nc.scalar.copy(
                wq_dealt[:, t : t + 2, :].rearrange("p t m -> p m t"),
                wq_w[:].bitcast(U32).rearrange("p (m t) -> p m t", t=PACK)[:, :, t : t + 2],
            )

        qv_ps = ps.tile([P, PACK, Q], F32, name="qv_ps", tag="first_and_last")
        for t in range(PACK):
            nc.tensor.matmul_mx(
                qv_ps[:, t, :],
                lhsT=wq_dealt[:, t, :].bitcast(FP8X4), lhsT_scale=wq_plane_dealt[:, t, :],
                rhs=st_codes[:].bitcast(FP8X4), rhs_scale=st_plane[:],
                start=True, stop=True,
            )

        nc.scalar.copy(arch_plane[0:4, :].bitcast(U32), arch_rows[:, 0, :].bitcast(U32))
        spread_scale_rows(arch_plane, arch_rows, first=1)
        c_ps = []
        for i in range(X // PIECE):
            cols = slice(i * PIECE, (i + 1) * PIECE)
            c_ps.append(ps.tile([P, PIECE], F32, name="c_ps%d" % i))
            nc.tensor.matmul_mx(
                c_ps[i][:],
                lhsT=st_codes[:].bitcast(FP8X4), lhsT_scale=st_plane[:],
                rhs=arch_w[:, 4 * cols.start : 4 * cols.stop].bitcast(FP8X4), rhs_scale=arch_plane[:, cols],
                start=True, stop=True,
            )
        spread_scale_rows(draft_plane, draft_rows)

        qv_bf = sb.tile([P, Q, PACK], BF16, name="qv_bf", align_bytes=64)
        nc.scalar.copy(qv_bf[:], qv_ps[:].rearrange("p t q -> p q t"))
        c_sb = scores.tile([P, X], F32, name="c_sb", offset=512)
        nc.vector.tensor_copy(c_sb[:, :PIECE], c_ps[0][:])
        nc.scalar.copy(c_sb[:, PIECE:], c_ps[1][:])
        qv_codes = scores.tile([P, Q], U32, name="qv_codes", offset=0, align_bytes=64)
        qv_plane = sb.tile([P, Q], U8, name="qv_plane", align_bytes=64)
        nc.vector.quantize_mx(qv_codes[:].bitcast(FP8X4), qv_plane[:], qv_bf[:].rearrange("p q t -> p (q t)"))

        w = sb.tile([P, SLOTS], F32, name="w")
        nc.vector.tensor_copy(w[:, 384:512], c_sb[:].indirect(list_c[:]))

        nc.scalar.activation(page[:].indirect(list_put[:, 24:32]), w[:, 384:512], COPY)

        b_sb = sb.tile([P, U], F32, name="b_sb")
        for i in range(U // PIECE):
            cols = slice(i * PIECE, (i + 1) * PIECE)
            b_ps = ps.tile([P, PIECE], F32, name="b_ps%d" % i)
            nc.tensor.matmul_mx(
                b_ps[:],
                lhsT=qv_codes[:].bitcast(FP8X4), lhsT_scale=qv_plane[:],
                rhs=draft_w[:, 2 * cols.start : 2 * cols.stop].bitcast(FP4X4), rhs_scale=draft_plane[:, cols],
                start=True, stop=True,
            )
            nc.vector.tensor_copy(b_sb[:, cols], b_ps[:])
        nc.vector.tensor_copy(w[:, 256:384], b_sb[:].indirect(list_b[:]))

        a_sb = sb.tile([P, T], F32, name="a_sb")
        for i in range(T // PIECE):
            cols = slice(i * PIECE, (i + 1) * PIECE)
            a_ps = ps.tile([P, PIECE], F32, name="a_ps%d" % i, tag="first_and_last" if i == 3 else "a_ps%d" % i)
            nc.tensor.matmul_mx(
                a_ps[:],
                lhsT=qv_codes[:].bitcast(FP8X4), lhsT_scale=qv_plane[:],
                rhs=(cache_w[:, 4 * cols.start : 4 * cols.stop] if i < 3 else cache_last_w[:]).bitcast(FP8X4), rhs_scale=cache_plane[4 * i :, :],
                start=True, stop=True,
            )
            if i in (1, 2):
                nc.scalar.copy(a_sb[:, cols], a_ps[:])
            else:
                nc.vector.tensor_copy(a_sb[:, cols], a_ps[:])
        nc.scalar.activation(page[:].indirect(list_put[:, 16:24]), w[:, 256:384], COPY)
        nc.vector.tensor_copy(w[:, 0:256], a_sb[:].indirect(list_a[:]))
        nc.scalar.activation(page[:].indirect(list_put[:, 0:16]), w[:, 0:256], COPY)

        got_lo = sb.tile([P, 256], F32, name="got_lo")
        got_hi = sb.tile([P, 256], F32, name="got_hi")
        nc.vector.tensor_copy(got_lo[:], page[:].indirect(list_get[:, 0:16]))
        nc.scalar.activation(got_hi[:], page[:].indirect(list_get[:, 16:32]), COPY)
        res_lo = sb.tile([P, 256], F32, name="res_lo")
        res_hi = sb.tile([P, 256], F32, name="res_hi")
        nc.vector.tensor_max(res_lo[:], got_lo[:], w[:, 0:256])
        nc.sync.dma_start(out[:, 0:256], res_lo[:])
        nc.vector.tensor_max(res_hi[:], got_hi[:], w[:, 256:512])
        nc.scalar.dma_start(out[:, 256:512], res_hi[:])
